import numpy as np
import ml_dtypes


def mxq(x, axis, fmt="e4m3"):
    dtype, down = {"e4m3": (ml_dtypes.float8_e4m3fn, 7), "e5m2": (ml_dtypes.float8_e5m2, 14)}[fmt]
    v = np.moveaxis(np.asarray(x, np.float32).astype(ml_dtypes.bfloat16).astype(np.float64), axis, -1)
    blocks = v.reshape(v.shape[:-1] + (-1, 32))
    amax = np.abs(blocks).max(-1, keepdims=True)
    byte = np.maximum(np.where(amax > 0, np.frexp(amax)[1] - 1 + 127, 0) - down, 1)
    scale = np.exp2(byte - 127.0)
    codes = (blocks / scale).astype(np.float32).astype(dtype).astype(np.float64)
    return np.moveaxis((codes * scale).reshape(v.shape), -1, axis)


WIDE = False


def mx_kscale(k):
    if not WIDE:
        return np.ones(k)
    levels = np.array([10, -10, 5, -5, 0])
    if k % 512:
        return np.exp2(np.random.permutation(np.resize(levels, k // 32))).repeat(32)
    a = np.empty((k // 512, 16))
    for p in range(k // 512):
        a[p, :8] = np.random.permutation(np.resize(levels, 8))
        for g in range(8):
            far = levels[np.abs(levels - a[p, g]) >= 10]
            a[p, g + 8] = far[np.random.randint(len(far))]
    return np.exp2(a.ravel()).repeat(32)


BF16 = ml_dtypes.bfloat16


def bf(x):
    return np.asarray(x, np.float32).astype(BF16)


def f64(x):
    return np.asarray(x).astype(np.float64)


E2M1 = np.array([0.0, 0.5, 1.0, 1.5, 2.0, 3.0, 4.0, 6.0, -0.0, -0.5, -1.0, -1.5, -2.0, -3.0, -4.0, -6.0])


def pack_weight(w, fmt):
    k, n = w.shape
    w = f64(bf(w)).reshape(k // 32, 32, n)
    amax = np.abs(w).max(1)
    if fmt == "e4m3":
        byte = np.frexp(amax)[1] - 1 + 127 - 7
    else:
        mant, ex = np.frexp(amax / 6.0)
        byte = np.where(mant > 0.5, ex, ex - 1) + 127
    byte = np.clip(np.where(amax > 0, byte, 1), 1, 254)
    scaled = (w * np.exp2(127.0 - byte)[:, None, :]).reshape(k, n).astype(np.float32)
    by_word = np.ascontiguousarray(scaled.reshape(k // 512, 128, 4, n).transpose(0, 1, 3, 2))
    if fmt == "e4m3":
        words = by_word.astype(ml_dtypes.float8_e4m3fn).view(np.uint8)
    else:
        c = by_word.astype(ml_dtypes.float4_e2m1fn).view(np.uint8) & 0xF
        words = c[..., 0::2] | (c[..., 1::2] << 4)
    return np.ascontiguousarray(words), np.ascontiguousarray(byte.astype(np.uint8).reshape(k // 512, 16, n))


def unpack_weight(words, scales, fmt):
    g, p, n, _ = words.shape
    if fmt == "e4m3":
        vals = np.ascontiguousarray(words).view(ml_dtypes.float8_e4m3fn).astype(np.float64)
    else:
        nib = np.empty((g, p, n, 4), np.uint8)
        nib[..., 0::2] = words & 0xF
        nib[..., 1::2] = words >> 4
        vals = E2M1[nib]
    vals = vals * np.repeat(np.exp2(scales.astype(np.float64) - 127.0), 8, axis=1)[..., None]
    return vals.transpose(0, 1, 3, 2).reshape(g * 512, n)
def pack4(w):
    words, scales = pack_weight(w, "e2m1")
    return words.reshape(words.shape[0], 128, -1), scales


def unpack4(words, scales):
    return unpack_weight(words.reshape(words.shape[0], 128, -1, 2), scales, "e2m1")


B, M, Q, R = 1024, 1024, 512, 1536


def draw0():
    s, u, t = mx_kscale(M), mx_kscale(Q), mx_kscale(R)
    e_eff_words, e_eff_scales = pack4(np.random.standard_normal((Q, R)) / np.sqrt(Q) / u[:, None])
    sto_words, sto_scales = pack4(np.random.standard_normal((R, M)) / np.sqrt(R) / t[:, None])
    return {"dmet": bf(np.random.standard_normal((B, M)) * s),
            "deff": bf(np.random.standard_normal((B, Q)) * u),
            "e_met": bf(np.random.standard_normal((M, R)) / np.sqrt(M) / s[:, None]),
            "e_eff_words": e_eff_words, "e_eff_scales": e_eff_scales,
            "flux": bf(np.exp(0.3 * np.random.standard_normal(R)) * t),
            "sto_words": sto_words, "sto_scales": sto_scales,
            "conc": bf(np.exp(0.3 * np.random.standard_normal(M)))}


def core(dmet, deff, e_met, e_eff_words, e_eff_scales, flux, sto_words, sto_scales, conc):
    rel = ((mxq(f64(dmet), 1, "e4m3") @ mxq(f64(e_met), 0, "e4m3"))
           + (mxq(f64(deff), 1, "e4m3") @ unpack4(e_eff_words, e_eff_scales)))
    dv = rel * f64(flux)
    net = mxq(dv, 1, "e4m3") @ unpack4(sto_words, sto_scales)
    return net / f64(conc)


def e4m3fn_bytes(y):
    return np.clip(np.asarray(y, np.float64), -448.0, 448.0).astype(np.float32).astype(ml_dtypes.float8_e4m3fn).view(np.uint8)


def e4m3fn_values(b):
    return np.asarray(b, np.uint8).view(ml_dtypes.float8_e4m3fn).astype(np.float64)


def setup_inputs():
    d = draw0()
    x0 = np.asarray(d['e_met']).astype(np.float64)
    s = (np.max(np.abs(x0), axis=(1,), keepdims=True) / 448.0).astype(np.float32)
    out = {}
    for k, v in d.items():
        if k == 'e_met':
            out['e_met_bytes'] = e4m3fn_bytes(x0 / s.astype(np.float64))
            out['e_met_scale'] = s
        else:
            out[k] = v
    return out


def reference(dmet, deff, e_met_bytes, e_met_scale, e_eff_words, e_eff_scales, flux, sto_words, sto_scales, conc):
    return core(dmet, deff, e4m3fn_values(e_met_bytes) * e_met_scale.astype(np.float64), e_eff_words, e_eff_scales, flux, sto_words, sto_scales, conc)

@@ -1,0 +1,377 @@
+from contextlib import ExitStack
+
+import concourse.mybir as mybir
+from concourse.masks import make_identity
+
+B, M, Q, R = 1024, 1024, 512, 1536
+P = 128
+FLOPS = 2 * B * R * (M + Q) + 2 * B * R * M
+
+F32 = mybir.dt.float32
+BF16 = mybir.dt.bfloat16
+U32 = mybir.dt.uint32
+I32 = mybir.dt.int32
+U8 = mybir.dt.uint8
+F8 = mybir.dt.float8_e4m3fn
+E4M3X4 = mybir.dt.float8_e4m3fn_x4
+E2M1X4 = mybir.dt.float4_e2m1fn_x4
+MULT = mybir.AluOpType.mult
+ADD = mybir.AluOpType.add
+COPY = mybir.ActivationFunctionType.Copy
+
+G = 3
+S_SHARE = 64
+
+
+def tile_metabolic_jacobian_action_s3_kernel(
+    tc, dmet, deff, e_met_bytes, e_met_scale, e_eff_words, e_eff_scales, flux, sto_words, sto_scales, conc, out
+):
+    nc = tc.nc
+    with ExitStack() as ctx:
+        keep = ctx.enter_context(tc.tile_pool(name="keep", bufs=1))
+        psum = ctx.enter_context(tc.psum_pool(name="psum", bufs=1))
+        ctx.enter_context(tc.manual_schedule())
+
+        def kept(name, shape, dtype):
+            return keep.tile(shape, dtype, name=name, tag=name, align_bytes=64)
+
+        ident = kept("ident", [P, P], F32)
+        dm = [kept(f"dm{h}", [P, 4, M], BF16) for h in range(2)]
+        df = [kept(f"df{h}", [P, 4, Q], BF16) for h in range(2)]
+        xg = [kept(f"xg{k}", [P, B, 2], F32) for k in range(3)]
+        xc = [kept(f"xc{k}", [P, B], U32) for k in range(3)]
+        xs = [kept(f"xs{k}", [P, B], U8) for k in range(3)]
+        eb0 = [kept(f"eb0{k}", [P, 4, 512], U8) for k in range(2)]
+        eb1 = [kept(f"eb1{k}", [P, 4, 1024], U8) for k in range(2)]
+        esc = kept("esc", [P, 2, 4], F32)
+        ec = [kept(f"ec{k}", [P, R], U32) for k in range(2)]
+        es = [kept(f"es{k}", [P, R], U8) for k in range(2)]
+        fw_raw = kept("fw_raw", [P, 2 * R], U8)
+        fs_raw = kept("fs_raw", [P, R], U8)
+        fw = kept("fw", [P, 2 * R], U8)
+        fs = kept("fs", [P, R], U8)
+        fx = kept("fx", [P, G, 4], BF16)
+        dv = [kept(f"dv{g}", [P, B, 4], BF16) for g in range(G)]
+        dc = [kept(f"dc{g}", [P, B], U32) for g in range(G)]
+        ds = [kept(f"ds{g}", [P, B], U8) for g in range(G)]
+        sw = kept("sw", [P, G, 2 * M], U8)
+        ss = kept("ss", [P, G, M], U8)
+        cc = kept("cc", [P, 8], BF16)
+        rcol = kept("rcol", [P, 8], F32)
+        rc = kept("rc", [P, M], F32)
+
+        make_identity(nc, ident[:])
+        nc.gpsimd.memset(fs_raw[:].bitcast(I32), 0)
+        nc.gpsimd.memset(ss[:].rearrange("p g n -> p (g n)").bitcast(I32), 0)
+        nc.scalar.dma_start(out=cc[:], in_=conc.rearrange("(p c) -> p c", c=8))
+        nc.scalar.dma_start(out=esc[:], in_=e_met_scale.rearrange("(k p t) o -> p k (t o)", p=P, t=4))
+        nc.scalar.dma_start(out=fx[:], in_=flux.rearrange("(g p t) -> p g t", p=P, t=4))
+
+        def load_dm(q):
+            h, c = q // 2, 2 * (q % 2)
+            nc.sync.dma_start(
+                out=dm[h][:, c : c + 2, :],
+                in_=dmet[512 * h : 512 * (h + 1), :].rearrange("(p c) k -> p c k", c=4)[:, c : c + 2, :],
+            )
+
+        def load_df(q):
+            h, c = q // 2, 2 * (q % 2)
+            nc.sync.dma_start(
+                out=df[h][:, c : c + 2, :],
+                in_=deff[512 * h : 512 * (h + 1), :].rearrange("(p c) k -> p c k", c=4)[:, c : c + 2, :],
+            )
+
+        def load_eb(tile, k, c0, c1):
+            nc.sync.dma_start(
+                out=tile[k][:],
+                in_=e_met_bytes[512 * k : 512 * (k + 1), c0:c1].rearrange("(p t) n -> p t n", t=4),
+            )
+
+        def load_fw():
+            nc.sync.dma_start(out=fw_raw[:], in_=e_eff_words[0])
+
+        def load_fs():
+            for q in range(4):
+                nc.sync.dma_start(
+                    out=fs_raw[32 * q : 32 * q + 4, :].bitcast(I32),
+                    in_=e_eff_scales[0][4 * q : 4 * q + 4, :].bitcast(I32),
+                )
+
+        def load_sto():
+            nc.sync.dma_start(out=sw[:], in_=sto_words.rearrange("g p n -> p g n"))
+            for q in range(4):
+                nc.sync.dma_start(
+                    out=ss[32 * q : 32 * q + 4, :, :].bitcast(I32),
+                    in_=sto_scales[:, 4 * q : 4 * q + 4, :].rearrange("g r n -> r g n").bitcast(I32),
+                )
+
+        load_eb(eb0, 0, 0, 512)
+        load_eb(eb0, 1, 0, 512)
+        load_dm(0)
+        load_df(0)
+        load_fw()
+        load_fs()
+        load_dm(1)
+        load_df(1)
+        load_eb(eb1, 0, 512, 1536)
+        load_dm(2)
+        load_df(2)
+        load_eb(eb1, 1, 512, 1536)
+        load_dm(3)
+        load_df(3)
+        load_sto()
+
+        def bank(i, shape):
+            return psum.tile(shape, F32, name=f"bank{i}", tag=f"bank{i}")
+
+        t_banks = {}
+
+        def t_in(q, k):
+            h, c = q // 2, 2 * (q % 2)
+            b = bank((3 * q + k) % 3, [P, 2, 2, P])
+            t_banks[q, k] = b
+            for i in range(2):
+                if k < 2:
+                    words = dm[h][:, c + i, 512 * k : 512 * (k + 1)].bitcast(F32)
+                else:
+                    words = df[h][:, c + i, :].bitcast(F32)
+                for u in range(2):
+                    nc.tensor.transpose(b[:, i, u, :], words[:, u:256:2], ident[:])
+
+        def t_out(q, k):
+            nc.scalar.copy(
+                out=xg[k][:, 256 * q : 256 * (q + 1), :].rearrange("p (i b) u -> p i b u", i=2),
+                in_=t_banks[q, k][:].rearrange("p i u b -> p i b u"),
+            )
+
+        def quant_x(q, k):
+            cols = slice(256 * q, 256 * (q + 1))
+            nc.vector.quantize_mx(
+                out=xc[k][:, cols].bitcast(E4M3X4),
+                scales=xs[k][:, cols],
+                in_=xg[k][:, cols, :].rearrange("p b u -> p (b u)").bitcast(BF16),
+            )
+
+        wide = {}
+        quads = {}
+
+        def widen(eng, g, k, t):
+            if (g, k) not in wide:
+                wide[g, k] = keep.tile([P, 4, 512], BF16, name=f"wide{k}{g % 2}", tag=f"wide{k}{g % 2}", align_bytes=64)
+            w = wide[g, k]
+            s = eb0[k][:, t, :] if g == 0 else eb1[k][:, t, 512 * (g - 1) : 512 * g]
+            if eng == "v":
+                nc.vector.tensor_scalar(
+                    out=w[:, t, :], in0=s.bitcast(F8), scalar1=esc[:, k, t : t + 1], scalar2=None, op0=MULT
+                )
+            else:
+                nc.scalar.activation(out=w[:, t, :], in_=s.bitcast(F8), func=COPY, scale=esc[:, k, t : t + 1])
+
+        def interleave(eng, g, k, m0, m1):
+            if (g, k) not in quads:
+                quads[g, k] = keep.tile([P, 512, 4], BF16, name=f"quads{k}{g % 2}", tag=f"quads{k}{g % 2}", align_bytes=64)
+            o = quads[g, k][:].rearrange("p (t m) j -> p m t j", t=4)[:, m0:m1]
+            i = wide[g, k][:].rearrange("p j (m t) -> p m t j", t=4)[:, m0:m1]
+            if eng == "v":
+                nc.vector.tensor_copy(out=o, in_=i)
+            elif eng == "g":
+                nc.gpsimd.tensor_scalar(out=o, in0=i, scalar1=1.0, scalar2=0.0, op0=MULT, op1=ADD)
+            else:
+                nc.scalar.copy(out=o, in_=i)
+
+        def quant_e(g, k):
+            cols = slice(512 * g, 512 * (g + 1))
+            nc.vector.quantize_mx(
+                out=ec[k][:, cols].bitcast(E4M3X4),
+                scales=es[k][:, cols],
+                in_=quads[g, k][:].rearrange("p c j -> p (c j)"),
+            )
+
+        def permute_words(g):
+            nc.vector.tensor_copy(
+                out=fw[:, 1024 * g : 1024 * (g + 1)].rearrange("p (t m e) -> p m t e", t=4, e=2),
+                in_=fw_raw[:, 1024 * g : 1024 * (g + 1)].rearrange("p (m t e) -> p m t e", t=4, e=2),
+            )
+
+        def permute_scales(g):
+            nc.vector.tensor_copy(
+                out=fs[:, 512 * g : 512 * (g + 1)].rearrange("p (t m) -> p m t", t=4),
+                in_=fs_raw[:, 512 * g : 512 * (g + 1)].rearrange("p (m t) -> p m t", t=4),
+            )
+
+        s_banks = {}
+
+        def s1(slot):
+            g, bt = slot // 8, slot % 8
+            b = bank(3 + slot % 5, [P, 4, P])
+            s_banks[slot] = b
+            rows = slice(P * bt, P * (bt + 1))
+            for t in range(4):
+                c0 = 512 * g + P * t
+                for k in range(3):
+                    if k < 2:
+                        lhs, lhs_s = ec[k][:, c0 : c0 + P].bitcast(E4M3X4), es[k][:, c0 : c0 + P]
+                    else:
+                        lhs, lhs_s = fw[:, 2 * c0 : 2 * (c0 + P)].bitcast(E2M1X4), fs[:, c0 : c0 + P]
+                    nc.tensor.matmul_mx(
+                        out=b[:, t, :],
+                        lhsT=lhs,
+                        lhsT_scale=lhs_s,
+                        rhs=xc[k][:, rows].bitcast(E4M3X4),
+                        rhs_scale=xs[k][:, rows],
+                        start=(k == 0),
+                        stop=(k == 2),
+                    )
+
+        def s1_out(slot):
+            g, bt = slot // 8, slot % 8
+            nc.vector.tensor_tensor(
+                out=dv[g][:, P * bt : P * (bt + 1), :],
+                in0=s_banks[slot][:].rearrange("p t b -> p b t"),
+                in1=fx[:, g, :].unsqueeze(1).to_broadcast([P, P, 4]),
+                op=MULT,
+            )
+
+        def quant_dv(g, b0, b1):
+            nc.vector.quantize_mx(
+                out=dc[g][:, b0:b1].bitcast(E4M3X4),
+                scales=ds[g][:, b0:b1],
+                in_=dv[g][:, b0:b1, :].rearrange("p b t -> p (b t)"),
+            )
+
+        o_banks = {}
+        results = {}
+
+        def s2(u, g):
+            bt, mh = u // 2, u % 2
+            if g == 0:
+                o_banks[u] = bank(u % 8, [P, 512])
+            rows = slice(P * bt, P * (bt + 1))
+            cols = slice(512 * mh, 512 * (mh + 1))
+            nc.tensor.matmul_mx(
+                out=o_banks[u][:],
+                lhsT=dc[g][:, rows].bitcast(E4M3X4),
+                lhsT_scale=ds[g][:, rows],
+                rhs=sw[:, g, 1024 * mh : 1024 * (mh + 1)].bitcast(E2M1X4),
+                rhs_scale=ss[:, g, cols],
+                start=(g == 0),
+                stop=(g == G - 1),
+            )
+
+        def s2_out(u):
+            bt, mh = u // 2, u % 2
+            h, c = bt // 4, bt % 4
+            if mh == 0:
+                results[bt] = keep.tile([P, M], F32, name=f"result{bt % 4}", tag=f"result{bt % 4}")
+            dst = out[512 * h : 512 * (h + 1), :].rearrange("(p c) m -> p c m", c=4)[:, c, :]
+            o = results[bt]
+            pieces = 2 if u == 15 else 1
+            for i in range(pieces):
+                c0 = 512 * mh + 512 // pieces * i
+                cols = slice(c0, c0 + 512 // pieces)
+                nc.vector.tensor_tensor(out=o[:, cols], in0=o_banks[u][:, c0 - 512 * mh : c0 - 512 * mh + 512 // pieces], in1=rc[:, cols], op=MULT)
+                if bt == 7:
+                    nc.sync.dma_start(out=dst[:, cols], in_=o[:, cols])
+            if bt < 7 and mh == 1:
+                nc.sync.dma_start(out=dst, in_=o[:])
+
+        def rc_col():
+            nc.vector.reciprocal(out=rcol[:], in_=cc[:])
+
+        def rc_spread():
+            nc.sync.dma_start(out=out[0:1, :].rearrange("o (p c) -> (o p) c", c=8), in_=rcol[:])
+            nc.sync.dma_start(out=rc[:], in_=out[0, :].partition_broadcast(P))
+
+
+        rc_col()
+        for k in range(2):
+            for t in range(4):
+                widen("vvss"[t], 0, k, t)
+        rc_spread()
+
+        def x_in(q):
+            for k in range(3):
+                t_in(q, k)
+            for k in range(3):
+                t_out(q, k)
+
+        def x_quant(q):
+            for k in range(3):
+                quant_x(q, k)
+
+        x_in(0)
+        interleave("v", 0, 0, 0, 128)
+        interleave("s", 0, 1, 0, 64)
+        permute_words(0)
+        quant_e(0, 0)
+        quant_x(0, 0)
+        interleave("v", 0, 1, 64, 128)
+        quant_x(0, 1)
+        permute_scales(0)
+        quant_e(0, 1)
+        quant_x(0, 2)
+        x_in(1)
+        s1(0)
+        s1(1)
+        for t in range(4):
+            widen("s", 1, 0, t)
+        x_quant(1)
+        s1_out(0)
+        permute_words(1)
+        s1_out(1)
+        x_in(2)
+        interleave("v", 1, 0, 0, 128)
+        for t in range(4):
+            widen("s", 1, 1, t)
+        s1(2)
+        s1(3)
+        permute_scales(1)
+        s1_out(2)
+        x_quant(2)
+        quant_e(1, 0)
+        s1_out(3)
+        x_in(3)
+        s1(4)
+        s1(5)
+        interleave("s", 1, 1, 0, 64)
+        interleave("v", 1, 1, 64, 128)
+        s1_out(4)
+        x_quant(3)
+        s1_out(5)
+        s1(6)
+        s1(7)
+        s1_out(6)
+        quant_e(1, 1)
+        s1_out(7)
+        for k in range(2):
+            for t in range(4):
+                widen("s", 2, k, t)
+            interleave("s", 2, k, 0, 96)
+        for slot in range(8, 16):
+            s1(slot)
+            s1_out(slot)
+            if slot == 8:
+                permute_words(2)
+            if slot == 9:
+                permute_scales(2)
+            if slot == 11:
+                interleave("v", 2, 0, 96, 128)
+            if slot == 13:
+                quant_e(2, 0)
+            if slot == 14:
+                interleave("v", 2, 1, 96, 128)
+        quant_e(2, 1)
+        for slot in range(16, 24):
+            s1(slot)
+            s1_out(slot)
+            if slot < 20:
+                quant_dv((slot - 16) % 2, 512 * ((slot - 16) // 2), 512 * ((slot - 16) // 2) + 512)
+            elif slot == 20:
+                quant_dv(2, 0, 512)
+            elif slot == 22:
+                quant_dv(2, 512, 768)
+        quant_dv(2, 768, 1024)
+        for u in range(16):
+            for g in range(G):
+                s2(u, g)
+            s2_out(u)

@@ -50,7 +50,9 @@ def tile_metabolic_jacobian_action_s3_kernel(
         fs_raw = kept("fs_raw", [P, R], U8)
         fw = kept("fw", [P, 2 * R], U8)
         fs = kept("fs", [P, R], U8)
-        fx = kept("fx", [P, G, 4], BF16)
+        fxb = kept("fxb", [P, G, 4], BF16)
+        fx = kept("fx", [P, G, 4], F32)
+        dvf = [kept(f"dvf{g}", [P, 4, B], BF16) for g in range(G)]
         dv = [kept(f"dv{g}", [P, B, 4], BF16) for g in range(G)]
         dc = [kept(f"dc{g}", [P, B], U32) for g in range(G)]
         ds = [kept(f"ds{g}", [P, B], U8) for g in range(G)]
@@ -65,7 +67,9 @@ def tile_metabolic_jacobian_action_s3_kernel(
         nc.gpsimd.memset(ss[:].rearrange("p g n -> p (g n)").bitcast(I32), 0)
         nc.scalar.dma_start(out=cc[:], in_=conc.rearrange("(p c) -> p c", c=8))
         nc.scalar.dma_start(out=esc[:], in_=e_met_scale.rearrange("(k p t) o -> p k (t o)", p=P, t=4))
-        nc.scalar.dma_start(out=fx[:], in_=flux.rearrange("(g p t) -> p g t", p=P, t=4))
+        nc.scalar.dma_start(out=fxb[:], in_=flux.rearrange("(g p t) -> p g t", p=P, t=4))
+
+        nc.gpsimd.tensor_copy(out=fx[:], in_=fxb[:])
 
         def load_dm(q):
             h, c = q // 2, 2 * (q % 2)
@@ -87,8 +91,8 @@ def tile_metabolic_jacobian_action_s3_kernel(
                 in_=e_met_bytes[512 * k : 512 * (k + 1), c0:c1].rearrange("(p t) n -> p t n", t=4),
             )
 
-        def load_fw():
-            nc.sync.dma_start(out=fw_raw[:], in_=e_eff_words[0])
+        def load_fw(c0, c1):
+            nc.sync.dma_start(out=fw_raw[:, 2 * c0 : 2 * c1], in_=e_eff_words[0][:, 2 * c0 : 2 * c1])
 
         def load_fs():
             for q in range(4):
@@ -105,20 +109,21 @@ def tile_metabolic_jacobian_action_s3_kernel(
                     in_=sto_scales[:, 4 * q : 4 * q + 4, :].rearrange("g r n -> r g n").bitcast(I32),
                 )
 
+        load_dm(0)
         load_eb(eb0, 0, 0, 512)
         load_eb(eb0, 1, 0, 512)
-        load_dm(0)
         load_df(0)
-        load_fw()
+        load_fw(0, 512)
         load_fs()
         load_dm(1)
         load_df(1)
-        load_eb(eb1, 0, 512, 1536)
         load_dm(2)
         load_df(2)
-        load_eb(eb1, 1, 512, 1536)
+        load_eb(eb1, 0, 512, 1536)
         load_dm(3)
         load_df(3)
+        load_eb(eb1, 1, 512, 1536)
+        load_fw(512, 1536)
         load_sto()
 
         def bank(i, shape):
@@ -138,11 +143,13 @@ def tile_metabolic_jacobian_action_s3_kernel(
                 for u in range(2):
                     nc.tensor.transpose(b[:, i, u, :], words[:, u:256:2], ident[:])
 
-        def t_out(q, k):
-            nc.scalar.copy(
-                out=xg[k][:, 256 * q : 256 * (q + 1), :].rearrange("p (i b) u -> p i b u", i=2),
-                in_=t_banks[q, k][:].rearrange("p i u b -> p i b u"),
-            )
+        def t_out(q, k, eng="s"):
+            o = xg[k][:, 256 * q : 256 * (q + 1), :].rearrange("p (i b) u -> p i b u", i=2)
+            i = t_banks[q, k][:].rearrange("p i u b -> p i b u")
+            if eng == "v":
+                nc.vector.tensor_copy(out=o, in_=i)
+            else:
+                nc.scalar.copy(out=o, in_=i)
 
         def quant_x(q, k):
             cols = slice(256 * q, 256 * (q + 1))
@@ -155,23 +162,42 @@ def tile_metabolic_jacobian_action_s3_kernel(
         wide = {}
         quads = {}
 
-        def widen(eng, g, k, t):
-            if (g, k) not in wide:
-                wide[g, k] = keep.tile([P, 4, 512], BF16, name=f"wide{k}{g % 2}", tag=f"wide{k}{g % 2}", align_bytes=64)
-            w = wide[g, k]
+        def e_src(g, k, t):
             s = eb0[k][:, t, :] if g == 0 else eb1[k][:, t, 512 * (g - 1) : 512 * g]
+            return s.bitcast(F8)
+
+        def e_tiles(g, k):
+            if (g, k) not in wide:
+                wide[g, k] = keep.tile([P, 2, 512], F32, name=f"wide{k}{g % 2}", tag=f"wide{k}{g % 2}", align_bytes=64)
+                quads[g, k] = keep.tile([P, 512, 2], F32, name=f"quads{k}{g % 2}", tag=f"quads{k}{g % 2}", align_bytes=64)
+            return wide[g, k], quads[g, k]
+
+        def widen_pairs(g, k, t):
+            w = e_tiles(g, k)[0][:, t // 2 : t // 2 + 1, :].rearrange("p v n -> p (v n)").bitcast(BF16).rearrange("p (n e) -> p n e", e=2)
+            nc.vector.tensor_scalar(
+                out=w[:, :, t % 2], in0=e_src(g, k, t), scalar1=esc[:, k, t : t + 1], scalar2=None, op0=MULT
+            )
+
+        def pair_up(eng, g, k, m0, m1):
+            w, q = e_tiles(g, k)
+            o = q[:].rearrange("p (t m) v -> p m t v", t=4)[:, m0:m1]
+            i = w[:].rearrange("p v (m t) -> p m t v", t=4)[:, m0:m1]
             if eng == "v":
-                nc.vector.tensor_scalar(
-                    out=w[:, t, :], in0=s.bitcast(F8), scalar1=esc[:, k, t : t + 1], scalar2=None, op0=MULT
-                )
+                nc.vector.tensor_copy(out=o, in_=i)
             else:
-                nc.scalar.activation(out=w[:, t, :], in_=s.bitcast(F8), func=COPY, scale=esc[:, k, t : t + 1])
+                nc.scalar.copy(out=o, in_=i)
+
+        def widen(eng, g, k, t):
+            w = e_tiles(g, k)[0][:, t // 2 : t // 2 + 1, :].rearrange("p v n -> p (v n)").bitcast(BF16)[:, 512 * (t % 2) : 512 * (t % 2 + 1)]
+            if eng == "v":
+                nc.vector.tensor_scalar(out=w, in0=e_src(g, k, t), scalar1=esc[:, k, t : t + 1], scalar2=None, op0=MULT)
+            else:
+                nc.scalar.activation(out=w, in_=e_src(g, k, t), func=COPY, scale=esc[:, k, t : t + 1])
 
         def interleave(eng, g, k, m0, m1):
-            if (g, k) not in quads:
-                quads[g, k] = keep.tile([P, 512, 4], BF16, name=f"quads{k}{g % 2}", tag=f"quads{k}{g % 2}", align_bytes=64)
-            o = quads[g, k][:].rearrange("p (t m) j -> p m t j", t=4)[:, m0:m1]
-            i = wide[g, k][:].rearrange("p j (m t) -> p m t j", t=4)[:, m0:m1]
+            w, q = e_tiles(g, k)
+            o = q[:].rearrange("p c v -> p (c v)").bitcast(BF16).rearrange("p (t m j) -> p m t j", t=4, j=4)[:, m0:m1]
+            i = w[:].rearrange("p v n -> p (v n)").bitcast(BF16).rearrange("p (j m t) -> p m t j", j=4, t=4)[:, m0:m1]
             if eng == "v":
                 nc.vector.tensor_copy(out=o, in_=i)
             elif eng == "g":
@@ -184,7 +210,7 @@ def tile_metabolic_jacobian_action_s3_kernel(
             nc.vector.quantize_mx(
                 out=ec[k][:, cols].bitcast(E4M3X4),
                 scales=es[k][:, cols],
-                in_=quads[g, k][:].rearrange("p c j -> p (c j)"),
+                in_=quads[g, k][:].rearrange("p c v -> p (c v)").bitcast(BF16),
             )
 
         def permute_words(g):
@@ -201,36 +227,42 @@ def tile_metabolic_jacobian_action_s3_kernel(
 
         s_banks = {}
 
-        def s1(slot):
-            g, bt = slot // 8, slot % 8
-            b = bank(3 + slot % 5, [P, 4, P])
-            s_banks[slot] = b
-            rows = slice(P * bt, P * (bt + 1))
-            for t in range(4):
-                c0 = 512 * g + P * t
-                for k in range(3):
-                    if k < 2:
-                        lhs, lhs_s = ec[k][:, c0 : c0 + P].bitcast(E4M3X4), es[k][:, c0 : c0 + P]
-                    else:
-                        lhs, lhs_s = fw[:, 2 * c0 : 2 * (c0 + P)].bitcast(E2M1X4), fs[:, c0 : c0 + P]
-                    nc.tensor.matmul_mx(
-                        out=b[:, t, :],
-                        lhsT=lhs,
-                        lhsT_scale=lhs_s,
-                        rhs=xc[k][:, rows].bitcast(E4M3X4),
-                        rhs_scale=xs[k][:, rows],
-                        start=(k == 0),
-                        stop=(k == 2),
-                    )
+        def s1(g, h, t):
+            n = 8 * g + 4 * h + t
+            b = bank(3 + n % 5, [P, 512])
+            s_banks[n] = b
+            rows = slice(512 * h, 512 * (h + 1))
+            c0 = 512 * g + P * t
+            for k in range(3):
+                if k < 2:
+                    lhs, lhs_s = ec[k][:, c0 : c0 + P].bitcast(E4M3X4), es[k][:, c0 : c0 + P]
+                else:
+                    lhs, lhs_s = fw[:, 2 * c0 : 2 * (c0 + P)].bitcast(E2M1X4), fs[:, c0 : c0 + P]
+                nc.tensor.matmul_mx(
+                    out=b[:],
+                    lhsT=lhs,
+                    lhsT_scale=lhs_s,
+                    rhs=xc[k][:, rows].bitcast(E4M3X4),
+                    rhs_scale=xs[k][:, rows],
+                    start=(k == 0),
+                    stop=(k == 2),
+                )
 
-        def s1_out(slot):
-            g, bt = slot // 8, slot % 8
-            nc.vector.tensor_tensor(
-                out=dv[g][:, P * bt : P * (bt + 1), :],
-                in0=s_banks[slot][:].rearrange("p t b -> p b t"),
-                in1=fx[:, g, :].unsqueeze(1).to_broadcast([P, P, 4]),
-                op=MULT,
-            )
+        def s1_out(eng, g, h, t):
+            b = s_banks[8 * g + 4 * h + t]
+            o = dvf[g][:, t, 512 * h : 512 * (h + 1)]
+            if eng == "v":
+                nc.vector.tensor_scalar(out=o, in0=b[:], scalar1=fx[:, g, t : t + 1], scalar2=None, op0=MULT)
+            else:
+                nc.scalar.activation(out=o, in_=b[:], func=COPY, scale=fx[:, g, t : t + 1])
+
+        def dv_in(eng, g, b0, b1):
+            o = dv[g][:, b0:b1, :]
+            i = dvf[g][:, :, b0:b1].rearrange("p t b -> p b t")
+            if eng == "v":
+                nc.vector.tensor_copy(out=o, in_=i)
+            else:
+                nc.scalar.copy(out=o, in_=i)
 
         def quant_dv(g, b0, b1):
             nc.vector.quantize_mx(
@@ -283,15 +315,11 @@ def tile_metabolic_jacobian_action_s3_kernel(
             nc.sync.dma_start(out=rc[:], in_=out[0, :].partition_broadcast(P))
 
 
-        rc_col()
-        for k in range(2):
-            for t in range(4):
-                widen("vvss"[t], 0, k, t)
-        rc_spread()
-
         def x_in(q):
             for k in range(3):
                 t_in(q, k)
+
+        def x_out(q):
             for k in range(3):
                 t_out(q, k)
 
@@ -299,79 +327,95 @@ def tile_metabolic_jacobian_action_s3_kernel(
             for k in range(3):
                 quant_x(q, k)
 
+        def pairs(g, k):
+            for t in range(4):
+                widen_pairs(g, k, t)
+
         x_in(0)
-        interleave("v", 0, 0, 0, 128)
-        interleave("s", 0, 1, 0, 64)
+        t_out(0, 0)
+        t_out(0, 1)
+        pairs(0, 0)
+        for t in range(4):
+            widen("s", 0, 1, t)
+        t_out(0, 2)
         permute_words(0)
-        quant_e(0, 0)
-        quant_x(0, 0)
-        interleave("v", 0, 1, 64, 128)
-        quant_x(0, 1)
         permute_scales(0)
-        quant_e(0, 1)
+        quant_x(0, 0)
+        quant_x(0, 1)
+        pair_up("s", 0, 0, 0, 128)
+        interleave("v", 0, 1, 0, 128)
         quant_x(0, 2)
         x_in(1)
-        s1(0)
-        s1(1)
-        for t in range(4):
-            widen("s", 1, 0, t)
+        x_out(1)
+        quant_e(0, 0)
+        quant_e(0, 1)
         x_quant(1)
-        s1_out(0)
-        permute_words(1)
-        s1_out(1)
         x_in(2)
-        interleave("v", 1, 0, 0, 128)
-        for t in range(4):
-            widen("s", 1, 1, t)
-        s1(2)
-        s1(3)
-        permute_scales(1)
-        s1_out(2)
-        x_quant(2)
-        quant_e(1, 0)
-        s1_out(3)
+        x_out(2)
+        rc_col()
+        rc_spread()
+        pairs(1, 0)
+        s1(0, 0, 0)
+        s1(0, 0, 1)
         x_in(3)
-        s1(4)
-        s1(5)
-        interleave("s", 1, 1, 0, 64)
-        interleave("v", 1, 1, 64, 128)
-        s1_out(4)
+        s1_out("s", 0, 0, 0)
+        x_out(3)
+        s1(0, 0, 2)
+        s1(0, 0, 3)
+        x_quant(2)
+        s1_out("s", 0, 0, 1)
+        widen_pairs(1, 1, 0)
+        widen_pairs(1, 1, 1)
+        pair_up("s", 1, 0, 0, 128)
         x_quant(3)
-        s1_out(5)
-        s1(6)
-        s1(7)
-        s1_out(6)
+        widen_pairs(1, 1, 2)
+        widen_pairs(1, 1, 3)
+        s1_out("v", 0, 0, 2)
+        s1_out("s", 0, 0, 3)
+        pair_up("s", 1, 1, 0, 128)
+        for t in range(4):
+            s1(0, 1, t)
+            s1_out("s", 0, 1, t)
+        permute_words(1)
+        permute_scales(1)
+        quant_e(1, 0)
         quant_e(1, 1)
-        s1_out(7)
         for k in range(2):
+            pairs(2, k)
+        permute_words(2)
+        permute_scales(2)
+        for h in range(2):
             for t in range(4):
-                widen("s", 2, k, t)
-            interleave("s", 2, k, 0, 96)
-        for slot in range(8, 16):
-            s1(slot)
-            s1_out(slot)
-            if slot == 8:
-                permute_words(2)
-            if slot == 9:
-                permute_scales(2)
-            if slot == 11:
-                interleave("v", 2, 0, 96, 128)
-            if slot == 13:
-                quant_e(2, 0)
-            if slot == 14:
-                interleave("v", 2, 1, 96, 128)
+                s1(1, h, t)
+                s1_out("s", 1, h, t)
+                if h == 0 and t % 2 == 0:
+                    pair_up("s", 2, t // 2, 0, 128)
+        quant_e(2, 0)
         quant_e(2, 1)
-        for slot in range(16, 24):
-            s1(slot)
-            s1_out(slot)
-            if slot < 20:
-                quant_dv((slot - 16) % 2, 512 * ((slot - 16) // 2), 512 * ((slot - 16) // 2) + 512)
-            elif slot == 20:
-                quant_dv(2, 0, 512)
-            elif slot == 22:
-                quant_dv(2, 512, 768)
-        quant_dv(2, 768, 1024)
+        dv_in("v", 0, 0, 512)
+        dv_in("v", 1, 0, 512)
+        quant_dv(0, 0, 512)
+        dv_in("v", 0, 512, 1024)
+        quant_dv(1, 0, 512)
+        for t in range(4):
+            s1(2, 0, t)
+            s1_out("s", 2, 0, t)
+        dv_in("s", 2, 0, 128)
+        dv_in("v", 2, 128, 512)
+        quant_dv(0, 512, 1024)
+        quant_dv(2, 0, 512)
+        dv_in("v", 1, 512, 1024)
+        for t in range(4):
+            s1(2, 1, t)
+            s1_out("s", 2, 1, t)
+        dv_in("s", 2, 512, 768)
         for u in range(16):
             for g in range(G):
                 s2(u, g)
             s2_out(u)
+            if u == 1:
+                quant_dv(1, 512, 1024)
+            if u == 2:
+                dv_in("v", 2, 768, 1024)
+            if u == 4:
+                quant_dv(2, 512, 1024)

from contextlib import ExitStack

import concourse.mybir as mybir
from concourse.masks import make_identity

B, M, Q, R = 1024, 1024, 512, 1536
P = 128
FLOPS = 2 * B * R * (M + Q) + 2 * B * R * M

F32 = mybir.dt.float32
BF16 = mybir.dt.bfloat16
U32 = mybir.dt.uint32
I32 = mybir.dt.int32
U8 = mybir.dt.uint8
F8 = mybir.dt.float8_e4m3fn
E4M3X4 = mybir.dt.float8_e4m3fn_x4
E2M1X4 = mybir.dt.float4_e2m1fn_x4
MULT = mybir.AluOpType.mult
ADD = mybir.AluOpType.add
COPY = mybir.ActivationFunctionType.Copy

G = 3
S_SHARE = 64


def tile_metabolic_jacobian_action_s3_kernel(
    tc, dmet, deff, e_met_bytes, e_met_scale, e_eff_words, e_eff_scales, flux, sto_words, sto_scales, conc, out
):
    nc = tc.nc
    with ExitStack() as ctx:
        keep = ctx.enter_context(tc.tile_pool(name="keep", bufs=1))
        psum = ctx.enter_context(tc.psum_pool(name="psum", bufs=1))
        ctx.enter_context(tc.manual_schedule())

        def kept(name, shape, dtype):
            return keep.tile(shape, dtype, name=name, tag=name, align_bytes=64)

        ident = kept("ident", [P, P], F32)
        dm = [kept(f"dm{h}", [P, 4, M], BF16) for h in range(2)]
        df = [kept(f"df{h}", [P, 4, Q], BF16) for h in range(2)]
        xg = [kept(f"xg{k}", [P, B, 2], F32) for k in range(3)]
        xc = [kept(f"xc{k}", [P, B], U32) for k in range(3)]
        xs = [kept(f"xs{k}", [P, B], U8) for k in range(3)]
        eb0 = [kept(f"eb0{k}", [P, 4, 512], U8) for k in range(2)]
        eb1 = [kept(f"eb1{k}", [P, 4, 1024], U8) for k in range(2)]
        esc = kept("esc", [P, 2, 4], F32)
        ec = [kept(f"ec{k}", [P, R], U32) for k in range(2)]
        es = [kept(f"es{k}", [P, R], U8) for k in range(2)]
        fw_raw = kept("fw_raw", [P, 2 * R], U8)
        fs_raw = kept("fs_raw", [P, R], U8)
        fw = kept("fw", [P, 2 * R], U8)
        fs = kept("fs", [P, R], U8)
        fxb = kept("fxb", [P, G, 4], BF16)
        fx = kept("fx", [P, G, 4], F32)
        dvf = [kept(f"dvf{g}", [P, 4, B], BF16) for g in range(G)]
        dv = [kept(f"dv{g}", [P, B, 4], BF16) for g in range(G)]
        dc = [kept(f"dc{g}", [P, B], U32) for g in range(G)]
        ds = [kept(f"ds{g}", [P, B], U8) for g in range(G)]
        sw = kept("sw", [P, G, 2 * M], U8)
        ss = kept("ss", [P, G, M], U8)
        cc = kept("cc", [P, 8], BF16)
        rcol = kept("rcol", [P, 8], F32)
        rc = kept("rc", [P, M], F32)

        make_identity(nc, ident[:])
        nc.gpsimd.memset(fs_raw[:].bitcast(I32), 0)
        nc.gpsimd.memset(ss[:].rearrange("p g n -> p (g n)").bitcast(I32), 0)
        nc.scalar.dma_start(out=cc[:], in_=conc.rearrange("(p c) -> p c", c=8))
        nc.scalar.dma_start(out=esc[:], in_=e_met_scale.rearrange("(k p t) o -> p k (t o)", p=P, t=4))
        nc.scalar.dma_start(out=fxb[:], in_=flux.rearrange("(g p t) -> p g t", p=P, t=4))

        nc.gpsimd.tensor_copy(out=fx[:], in_=fxb[:])

        def load_dm(q):
            h, c = q // 2, 2 * (q % 2)
            nc.sync.dma_start(
                out=dm[h][:, c : c + 2, :],
                in_=dmet[512 * h : 512 * (h + 1), :].rearrange("(p c) k -> p c k", c=4)[:, c : c + 2, :],
            )

        def load_df(q):
            h, c = q // 2, 2 * (q % 2)
            nc.sync.dma_start(
                out=df[h][:, c : c + 2, :],
                in_=deff[512 * h : 512 * (h + 1), :].rearrange("(p c) k -> p c k", c=4)[:, c : c + 2, :],
            )

        def load_eb(tile, k, c0, c1):
            nc.sync.dma_start(
                out=tile[k][:],
                in_=e_met_bytes[512 * k : 512 * (k + 1), c0:c1].rearrange("(p t) n -> p t n", t=4),
            )

        def load_fw(c0, c1):
            nc.sync.dma_start(out=fw_raw[:, 2 * c0 : 2 * c1], in_=e_eff_words[0][:, 2 * c0 : 2 * c1])

        def load_fs():
            for q in range(4):
                nc.sync.dma_start(
                    out=fs_raw[32 * q : 32 * q + 4, :].bitcast(I32),
                    in_=e_eff_scales[0][4 * q : 4 * q + 4, :].bitcast(I32),
                )

        def load_sto():
            nc.sync.dma_start(out=sw[:], in_=sto_words.rearrange("g p n -> p g n"))
            for q in range(4):
                nc.sync.dma_start(
                    out=ss[32 * q : 32 * q + 4, :, :].bitcast(I32),
                    in_=sto_scales[:, 4 * q : 4 * q + 4, :].rearrange("g r n -> r g n").bitcast(I32),
                )

        load_dm(0)
        load_eb(eb0, 0, 0, 512)
        load_eb(eb0, 1, 0, 512)
        load_df(0)
        load_fw(0, 512)
        load_fs()
        load_dm(1)
        load_df(1)
        load_dm(2)
        load_df(2)
        load_eb(eb1, 0, 512, 1536)
        load_dm(3)
        load_df(3)
        load_eb(eb1, 1, 512, 1536)
        load_fw(512, 1536)
        load_sto()

        def bank(i, shape):
            return psum.tile(shape, F32, name=f"bank{i}", tag=f"bank{i}")

        t_banks = {}

        def t_in(q, k):
            h, c = q // 2, 2 * (q % 2)
            b = bank((3 * q + k) % 3, [P, 2, 2, P])
            t_banks[q, k] = b
            for i in range(2):
                if k < 2:
                    words = dm[h][:, c + i, 512 * k : 512 * (k + 1)].bitcast(F32)
                else:
                    words = df[h][:, c + i, :].bitcast(F32)
                for u in range(2):
                    nc.tensor.transpose(b[:, i, u, :], words[:, u:256:2], ident[:])

        def t_out(q, k, eng="s"):
            o = xg[k][:, 256 * q : 256 * (q + 1), :].rearrange("p (i b) u -> p i b u", i=2)
            i = t_banks[q, k][:].rearrange("p i u b -> p i b u")
            if eng == "v":
                nc.vector.tensor_copy(out=o, in_=i)
            else:
                nc.scalar.copy(out=o, in_=i)

        def quant_x(q, k):
            cols = slice(256 * q, 256 * (q + 1))
            nc.vector.quantize_mx(
                out=xc[k][:, cols].bitcast(E4M3X4),
                scales=xs[k][:, cols],
                in_=xg[k][:, cols, :].rearrange("p b u -> p (b u)").bitcast(BF16),
            )

        wide = {}
        quads = {}

        def e_src(g, k, t):
            s = eb0[k][:, t, :] if g == 0 else eb1[k][:, t, 512 * (g - 1) : 512 * g]
            return s.bitcast(F8)

        def e_tiles(g, k):
            if (g, k) not in wide:
                wide[g, k] = keep.tile([P, 2, 512], F32, name=f"wide{k}{g % 2}", tag=f"wide{k}{g % 2}", align_bytes=64)
                quads[g, k] = keep.tile([P, 512, 2], F32, name=f"quads{k}{g % 2}", tag=f"quads{k}{g % 2}", align_bytes=64)
            return wide[g, k], quads[g, k]

        def widen_pairs(g, k, t):
            w = e_tiles(g, k)[0][:, t // 2 : t // 2 + 1, :].rearrange("p v n -> p (v n)").bitcast(BF16).rearrange("p (n e) -> p n e", e=2)
            nc.vector.tensor_scalar(
                out=w[:, :, t % 2], in0=e_src(g, k, t), scalar1=esc[:, k, t : t + 1], scalar2=None, op0=MULT
            )

        def pair_up(eng, g, k, m0, m1):
            w, q = e_tiles(g, k)
            o = q[:].rearrange("p (t m) v -> p m t v", t=4)[:, m0:m1]
            i = w[:].rearrange("p v (m t) -> p m t v", t=4)[:, m0:m1]
            if eng == "v":
                nc.vector.tensor_copy(out=o, in_=i)
            else:
                nc.scalar.copy(out=o, in_=i)

        def widen(eng, g, k, t):
            w = e_tiles(g, k)[0][:, t // 2 : t // 2 + 1, :].rearrange("p v n -> p (v n)").bitcast(BF16)[:, 512 * (t % 2) : 512 * (t % 2 + 1)]
            if eng == "v":
                nc.vector.tensor_scalar(out=w, in0=e_src(g, k, t), scalar1=esc[:, k, t : t + 1], scalar2=None, op0=MULT)
            else:
                nc.scalar.activation(out=w, in_=e_src(g, k, t), func=COPY, scale=esc[:, k, t : t + 1])

        def interleave(eng, g, k, m0, m1):
            w, q = e_tiles(g, k)
            o = q[:].rearrange("p c v -> p (c v)").bitcast(BF16).rearrange("p (t m j) -> p m t j", t=4, j=4)[:, m0:m1]
            i = w[:].rearrange("p v n -> p (v n)").bitcast(BF16).rearrange("p (j m t) -> p m t j", j=4, t=4)[:, m0:m1]
            if eng == "v":
                nc.vector.tensor_copy(out=o, in_=i)
            elif eng == "g":
                nc.gpsimd.tensor_scalar(out=o, in0=i, scalar1=1.0, scalar2=0.0, op0=MULT, op1=ADD)
            else:
                nc.scalar.copy(out=o, in_=i)

        def quant_e(g, k):
            cols = slice(512 * g, 512 * (g + 1))
            nc.vector.quantize_mx(
                out=ec[k][:, cols].bitcast(E4M3X4),
                scales=es[k][:, cols],
                in_=quads[g, k][:].rearrange("p c v -> p (c v)").bitcast(BF16),
            )

        def permute_words(g):
            nc.vector.tensor_copy(
                out=fw[:, 1024 * g : 1024 * (g + 1)].rearrange("p (t m e) -> p m t e", t=4, e=2),
                in_=fw_raw[:, 1024 * g : 1024 * (g + 1)].rearrange("p (m t e) -> p m t e", t=4, e=2),
            )

        def permute_scales(g):
            nc.vector.tensor_copy(
                out=fs[:, 512 * g : 512 * (g + 1)].rearrange("p (t m) -> p m t", t=4),
                in_=fs_raw[:, 512 * g : 512 * (g + 1)].rearrange("p (m t) -> p m t", t=4),
            )

        s_banks = {}

        def s1(g, h, t):
            n = 8 * g + 4 * h + t
            b = bank(3 + n % 5, [P, 512])
            s_banks[n] = b
            rows = slice(512 * h, 512 * (h + 1))
            c0 = 512 * g + P * t
            for k in range(3):
                if k < 2:
                    lhs, lhs_s = ec[k][:, c0 : c0 + P].bitcast(E4M3X4), es[k][:, c0 : c0 + P]
                else:
                    lhs, lhs_s = fw[:, 2 * c0 : 2 * (c0 + P)].bitcast(E2M1X4), fs[:, c0 : c0 + P]
                nc.tensor.matmul_mx(
                    out=b[:],
                    lhsT=lhs,
                    lhsT_scale=lhs_s,
                    rhs=xc[k][:, rows].bitcast(E4M3X4),
                    rhs_scale=xs[k][:, rows],
                    start=(k == 0),
                    stop=(k == 2),
                )

        def s1_out(eng, g, h, t):
            b = s_banks[8 * g + 4 * h + t]
            o = dvf[g][:, t, 512 * h : 512 * (h + 1)]
            if eng == "v":
                nc.vector.tensor_scalar(out=o, in0=b[:], scalar1=fx[:, g, t : t + 1], scalar2=None, op0=MULT)
            else:
                nc.scalar.activation(out=o, in_=b[:], func=COPY, scale=fx[:, g, t : t + 1])

        def dv_in(eng, g, b0, b1):
            o = dv[g][:, b0:b1, :]
            i = dvf[g][:, :, b0:b1].rearrange("p t b -> p b t")
            if eng == "v":
                nc.vector.tensor_copy(out=o, in_=i)
            else:
                nc.scalar.copy(out=o, in_=i)

        def quant_dv(g, b0, b1):
            nc.vector.quantize_mx(
                out=dc[g][:, b0:b1].bitcast(E4M3X4),
                scales=ds[g][:, b0:b1],
                in_=dv[g][:, b0:b1, :].rearrange("p b t -> p (b t)"),
            )

        o_banks = {}
        results = {}

        def s2(u, g):
            bt, mh = u // 2, u % 2
            if g == 0:
                o_banks[u] = bank(u % 8, [P, 512])
            rows = slice(P * bt, P * (bt + 1))
            cols = slice(512 * mh, 512 * (mh + 1))
            nc.tensor.matmul_mx(
                out=o_banks[u][:],
                lhsT=dc[g][:, rows].bitcast(E4M3X4),
                lhsT_scale=ds[g][:, rows],
                rhs=sw[:, g, 1024 * mh : 1024 * (mh + 1)].bitcast(E2M1X4),
                rhs_scale=ss[:, g, cols],
                start=(g == 0),
                stop=(g == G - 1),
            )

        def s2_out(u):
            bt, mh = u // 2, u % 2
            h, c = bt // 4, bt % 4
            if mh == 0:
                results[bt] = keep.tile([P, M], F32, name=f"result{bt % 4}", tag=f"result{bt % 4}")
            dst = out[512 * h : 512 * (h + 1), :].rearrange("(p c) m -> p c m", c=4)[:, c, :]
            o = results[bt]
            pieces = 2 if u == 15 else 1
            for i in range(pieces):
                c0 = 512 * mh + 512 // pieces * i
                cols = slice(c0, c0 + 512 // pieces)
                nc.vector.tensor_tensor(out=o[:, cols], in0=o_banks[u][:, c0 - 512 * mh : c0 - 512 * mh + 512 // pieces], in1=rc[:, cols], op=MULT)
                if bt == 7:
                    nc.sync.dma_start(out=dst[:, cols], in_=o[:, cols])
            if bt < 7 and mh == 1:
                nc.sync.dma_start(out=dst, in_=o[:])

        def rc_col():
            nc.vector.reciprocal(out=rcol[:], in_=cc[:])

        def rc_spread():
            nc.sync.dma_start(out=out[0:1, :].rearrange("o (p c) -> (o p) c", c=8), in_=rcol[:])
            nc.sync.dma_start(out=rc[:], in_=out[0, :].partition_broadcast(P))


        def x_in(q):
            for k in range(3):
                t_in(q, k)

        def x_out(q):
            for k in range(3):
                t_out(q, k)

        def x_quant(q):
            for k in range(3):
                quant_x(q, k)

        def pairs(g, k):
            for t in range(4):
                widen_pairs(g, k, t)

        x_in(0)
        t_out(0, 0)
        t_out(0, 1)
        pairs(0, 0)
        for t in range(4):
            widen("s", 0, 1, t)
        t_out(0, 2)
        permute_words(0)
        permute_scales(0)
        quant_x(0, 0)
        quant_x(0, 1)
        pair_up("s", 0, 0, 0, 128)
        interleave("v", 0, 1, 0, 128)
        quant_x(0, 2)
        x_in(1)
        x_out(1)
        quant_e(0, 0)
        quant_e(0, 1)
        x_quant(1)
        x_in(2)
        x_out(2)
        rc_col()
        rc_spread()
        pairs(1, 0)
        s1(0, 0, 0)
        s1(0, 0, 1)
        x_in(3)
        s1_out("s", 0, 0, 0)
        x_out(3)
        s1(0, 0, 2)
        s1(0, 0, 3)
        x_quant(2)
        s1_out("s", 0, 0, 1)
        widen_pairs(1, 1, 0)
        widen_pairs(1, 1, 1)
        pair_up("s", 1, 0, 0, 128)
        x_quant(3)
        widen_pairs(1, 1, 2)
        widen_pairs(1, 1, 3)
        s1_out("v", 0, 0, 2)
        s1_out("s", 0, 0, 3)
        pair_up("s", 1, 1, 0, 128)
        for t in range(4):
            s1(0, 1, t)
            s1_out("s", 0, 1, t)
        permute_words(1)
        permute_scales(1)
        quant_e(1, 0)
        quant_e(1, 1)
        for k in range(2):
            pairs(2, k)
        permute_words(2)
        permute_scales(2)
        for h in range(2):
            for t in range(4):
                s1(1, h, t)
                s1_out("s", 1, h, t)
                if h == 0 and t % 2 == 0:
                    pair_up("s", 2, t // 2, 0, 128)
        quant_e(2, 0)
        quant_e(2, 1)
        dv_in("v", 0, 0, 512)
        dv_in("v", 1, 0, 512)
        quant_dv(0, 0, 512)
        dv_in("v", 0, 512, 1024)
        quant_dv(1, 0, 512)
        for t in range(4):
            s1(2, 0, t)
            s1_out("s", 2, 0, t)
        dv_in("s", 2, 0, 128)
        dv_in("v", 2, 128, 512)
        quant_dv(0, 512, 1024)
        quant_dv(2, 0, 512)
        dv_in("v", 1, 512, 1024)
        for t in range(4):
            s1(2, 1, t)
            s1_out("s", 2, 1, t)
        dv_in("s", 2, 512, 768)
        for u in range(16):
            for g in range(G):
                s2(u, g)
            s2_out(u)
            if u == 1:
                quant_dv(1, 512, 1024)
            if u == 2:
                dv_in("v", 2, 768, 1024)
            if u == 4:
                quant_dv(2, 512, 1024)
